import numpy as np
import ml_dtypes

BF16 = ml_dtypes.bfloat16


def bf(x):
    return np.asarray(x, np.float32).astype(BF16)


def f32(x):
    return np.asarray(x, np.float32)


def f64(x):
    return np.asarray(x).astype(np.float64)


def striped(idx):
    return np.tile(idx.reshape(-1, 16).T, (8, 1))


S, K, M, N, D, V = 2048, 128, 512, 512, 16, 32


def setup_inputs():
    return {"table": bf(np.random.standard_normal((S, K))), "w": bf(np.random.standard_normal((K, M)) / np.sqrt(K)), "b": f32(0.5 * np.random.standard_normal((M, 1))), "offs": striped(np.random.permutation(S)[:N])}


def reference(table, w, b, offs):
    idx = offs[:16].T.reshape(-1)
    x = f64(table)[idx].T
    y = f64(w).T @ x
    z = np.tanh(y + f64(b))
    return z.reshape(M, V, D).max(axis=2)

@@ -1,0 +1,89 @@
+import concourse.mybir as mybir
+from concourse.masks import make_identity
+
+S, K, M, N = 2048, 128, 512, 512
+NEIGHBOURS = 16
+POOLED = N // NEIGHBOURS
+P = 128
+BLOCKS = M // P
+LOADS = ((1, 4), (1, 4), (2, 2), (2, 2))
+LINE = 4
+PIECE = 256
+TAIL = 64
+FLOPS = 2 * K * M * N
+
+BF16, F32, U16 = mybir.dt.bfloat16, mybir.dt.float32, mybir.dt.uint16
+TANH = mybir.ActivationFunctionType.Tanh
+
+
+def tile_gather_matmul_kernel(tc, table, w, b, offs, out):
+    nc = tc.nc
+    with (
+        tc.tile_pool(name="held", bufs=1) as held,
+        tc.tile_pool(name="pooled", bufs=BLOCKS) as pooled_pool,
+        tc.psum_pool(name="banks", bufs=8) as banks,
+    ):
+        identity = held.tile([P, P], BF16, name="identity")
+        make_identity(nc, identity[:])
+
+        groups = []
+        first_node = 0
+        for count, run in LOADS:
+            nodes = count * run * P
+            loaded = held.tile([P, count, run, K], BF16, name=f"loaded{first_node}")
+            nc.sync.dma_start(
+                loaded[:], table[first_node:first_node + nodes, :].rearrange("(g p r) k -> p g r k", p=P, r=run),
+            )
+            groups.extend((loaded[:, g], first_node + g * run * P, run) for g in range(count))
+            first_node += nodes
+        offsets = held.tile([P, N // 16], U16, name="offsets")
+        nc.sync.dma_start(offsets[:], offs)
+        weights = held.tile([K, P, BLOCKS], BF16, name="weights")
+        nc.sync.dma_start(weights[:], w.rearrange("k (p a) -> k p a", a=BLOCKS))
+        bias = held.tile([P, BLOCKS], F32, name="bias")
+        nc.sync.dma_start(bias[:], b.rearrange("(p a) o -> p (a o)", a=BLOCKS))
+
+        window = held.tile([K, S], BF16, name="window")
+        for g, (group, first_node, run) in enumerate(groups):
+            flipped = banks.tile([K, run, P], BF16, name="flipped", tag="bank")
+            for r in range(run):
+                nc.tensor.transpose(flipped[:, r, :], group[:, r, :], identity[:])
+            source = flipped[:].rearrange("k r (q i) -> k q r i", i=LINE)
+            target = window[:, first_node:first_node + run * P].rearrange("k (q i r) -> k q r i", i=LINE, r=run)
+            if g % 2 == 0:
+                nc.vector.tensor_copy(target, source)
+            else:
+                nc.scalar.copy(target, source)
+
+        def project(a, first, last):
+            product = banks.tile([P, last - first], F32, name="product", tag="bank")
+            nc.tensor.matmul(
+                product[:], weights[:, :, a], window[:].indirect(offsets[:, first // 16:last // 16]),
+                start=True, stop=True,
+            )
+            return product
+
+        def pool(target, first, last, values):
+            nc.vector.reduce_max(
+                target[:, first // NEIGHBOURS:last // NEIGHBOURS],
+                values[:].rearrange("p (v t) -> p v t", t=NEIGHBOURS), axis=mybir.AxisListType.X,
+            )
+
+        rows = out.rearrange("(p a) v -> p a v", a=BLOCKS)
+        early = held.tile([P, BLOCKS - 1, POOLED], F32, name="early")
+        late = held.tile([P, POOLED], F32, name="late")
+        for a in range(BLOCKS):
+            pooled_first = N - TAIL if a == BLOCKS - 1 else N
+            largest = pooled_pool.tile([P, POOLED], F32, name="largest")
+            result = late[:] if a == BLOCKS - 1 else early[:, a, :]
+            for first in range(0, pooled_first, PIECE):
+                last = min(first + PIECE, pooled_first)
+                pool(largest, first, last, project(a, first, last))
+            if pooled_first < N:
+                activated = held.tile([P, TAIL], F32, name="activated")
+                nc.scalar.activation(activated[:], project(a, pooled_first, N)[:], TANH, bias=bias[:, a:a + 1])
+                pool(result, pooled_first, N, activated)
+            columns = slice(0, pooled_first // NEIGHBOURS)
+            nc.scalar.activation(result[:, columns], largest[:, columns], TANH, bias=bias[:, a:a + 1])
+        nc.sync.dma_start(rows[:, :BLOCKS - 1, :], early[:])
+        nc.sync.dma_start(rows[:, BLOCKS - 1, :], late[:])

@@ -7,7 +7,6 @@ POOLED = N // NEIGHBOURS
 P = 128
 BLOCKS = M // P
 LOADS = ((1, 4), (1, 4), (2, 2), (2, 2))
-LINE = 4
 PIECE = 256
 TAIL = 64
 FLOPS = 2 * K * M * N
@@ -23,6 +22,11 @@ def tile_gather_matmul_kernel(tc, table, w, b, offs, out):
         tc.tile_pool(name="pooled", bufs=BLOCKS) as pooled_pool,
         tc.psum_pool(name="banks", bufs=8) as banks,
     ):
+        zeros = held.tile([P, P], F32, name="zeros")
+        nc.gpsimd.memset(zeros[:], 0.0)
+        unread = banks.tile([P, 4, P], F32, name="unread", tag="bank")
+        nc.tensor.matmul(unread[:], zeros[:], zeros[:].unsqueeze(1).to_broadcast([P, 4, P]), start=True, stop=True)
+
         identity = held.tile([P, P], BF16, name="identity")
         make_identity(nc, identity[:])
 
@@ -48,8 +52,8 @@ def tile_gather_matmul_kernel(tc, table, w, b, offs, out):
             flipped = banks.tile([K, run, P], BF16, name="flipped", tag="bank")
             for r in range(run):
                 nc.tensor.transpose(flipped[:, r, :], group[:, r, :], identity[:])
-            source = flipped[:].rearrange("k r (q i) -> k q r i", i=LINE)
-            target = window[:, first_node:first_node + run * P].rearrange("k (q i r) -> k q r i", i=LINE, r=run)
+            source = flipped[:].rearrange("k r p -> k p r")
+            target = window[:, first_node:first_node + run * P].rearrange("k (p r) -> k p r", r=run)
             if g % 2 == 0:
                 nc.vector.tensor_copy(target, source)
             else:

import concourse.mybir as mybir
from concourse.masks import make_identity

S, K, M, N = 2048, 128, 512, 512
NEIGHBOURS = 16
POOLED = N // NEIGHBOURS
P = 128
BLOCKS = M // P
LOADS = ((1, 4), (1, 4), (2, 2), (2, 2))
PIECE = 256
TAIL = 64
FLOPS = 2 * K * M * N

BF16, F32, U16 = mybir.dt.bfloat16, mybir.dt.float32, mybir.dt.uint16
TANH = mybir.ActivationFunctionType.Tanh


def tile_gather_matmul_kernel(tc, table, w, b, offs, out):
    nc = tc.nc
    with (
        tc.tile_pool(name="held", bufs=1) as held,
        tc.tile_pool(name="pooled", bufs=BLOCKS) as pooled_pool,
        tc.psum_pool(name="banks", bufs=8) as banks,
    ):
        zeros = held.tile([P, P], F32, name="zeros")
        nc.gpsimd.memset(zeros[:], 0.0)
        unread = banks.tile([P, 4, P], F32, name="unread", tag="bank")
        nc.tensor.matmul(unread[:], zeros[:], zeros[:].unsqueeze(1).to_broadcast([P, 4, P]), start=True, stop=True)

        identity = held.tile([P, P], BF16, name="identity")
        make_identity(nc, identity[:])

        groups = []
        first_node = 0
        for count, run in LOADS:
            nodes = count * run * P
            loaded = held.tile([P, count, run, K], BF16, name=f"loaded{first_node}")
            nc.sync.dma_start(
                loaded[:], table[first_node:first_node + nodes, :].rearrange("(g p r) k -> p g r k", p=P, r=run),
            )
            groups.extend((loaded[:, g], first_node + g * run * P, run) for g in range(count))
            first_node += nodes
        offsets = held.tile([P, N // 16], U16, name="offsets")
        nc.sync.dma_start(offsets[:], offs)
        weights = held.tile([K, P, BLOCKS], BF16, name="weights")
        nc.sync.dma_start(weights[:], w.rearrange("k (p a) -> k p a", a=BLOCKS))
        bias = held.tile([P, BLOCKS], F32, name="bias")
        nc.sync.dma_start(bias[:], b.rearrange("(p a) o -> p (a o)", a=BLOCKS))

        window = held.tile([K, S], BF16, name="window")
        for g, (group, first_node, run) in enumerate(groups):
            flipped = banks.tile([K, run, P], BF16, name="flipped", tag="bank")
            for r in range(run):
                nc.tensor.transpose(flipped[:, r, :], group[:, r, :], identity[:])
            source = flipped[:].rearrange("k r p -> k p r")
            target = window[:, first_node:first_node + run * P].rearrange("k (p r) -> k p r", r=run)
            if g % 2 == 0:
                nc.vector.tensor_copy(target, source)
            else:
                nc.scalar.copy(target, source)

        def project(a, first, last):
            product = banks.tile([P, last - first], F32, name="product", tag="bank")
            nc.tensor.matmul(
                product[:], weights[:, :, a], window[:].indirect(offsets[:, first // 16:last // 16]),
                start=True, stop=True,
            )
            return product

        def pool(target, first, last, values):
            nc.vector.reduce_max(
                target[:, first // NEIGHBOURS:last // NEIGHBOURS],
                values[:].rearrange("p (v t) -> p v t", t=NEIGHBOURS), axis=mybir.AxisListType.X,
            )

        rows = out.rearrange("(p a) v -> p a v", a=BLOCKS)
        early = held.tile([P, BLOCKS - 1, POOLED], F32, name="early")
        late = held.tile([P, POOLED], F32, name="late")
        for a in range(BLOCKS):
            pooled_first = N - TAIL if a == BLOCKS - 1 else N
            largest = pooled_pool.tile([P, POOLED], F32, name="largest")
            result = late[:] if a == BLOCKS - 1 else early[:, a, :]
            for first in range(0, pooled_first, PIECE):
                last = min(first + PIECE, pooled_first)
                pool(largest, first, last, project(a, first, last))
            if pooled_first < N:
                activated = held.tile([P, TAIL], F32, name="activated")
                nc.scalar.activation(activated[:], project(a, pooled_first, N)[:], TANH, bias=bias[:, a:a + 1])
                pool(result, pooled_first, N, activated)
            columns = slice(0, pooled_first // NEIGHBOURS)
            nc.scalar.activation(result[:, columns], largest[:, columns], TANH, bias=bias[:, a:a + 1])
        nc.sync.dma_start(rows[:, :BLOCKS - 1, :], early[:])
        nc.sync.dma_start(rows[:, BLOCKS - 1, :], late[:])
